import numpy as np
import ml_dtypes


def mxq(x, axis, fmt="e4m3"):
    dtype, down = {"e4m3": (ml_dtypes.float8_e4m3fn, 7), "e5m2": (ml_dtypes.float8_e5m2, 14)}[fmt]
    v = np.moveaxis(np.asarray(x, np.float32).astype(ml_dtypes.bfloat16).astype(np.float64), axis, -1)
    blocks = v.reshape(v.shape[:-1] + (-1, 32))
    amax = np.abs(blocks).max(-1, keepdims=True)
    byte = np.maximum(np.where(amax > 0, np.frexp(amax)[1] - 1 + 127, 0) - down, 1)
    scale = np.exp2(byte - 127.0)
    codes = (blocks / scale).astype(np.float32).astype(dtype).astype(np.float64)
    return np.moveaxis((codes * scale).reshape(v.shape), -1, axis)


WIDE = False


def mx_kscale(k):
    if not WIDE:
        return np.ones(k)
    levels = np.array([10, -10, 5, -5, 0])
    if k % 512:
        return np.exp2(np.random.permutation(np.resize(levels, k // 32))).repeat(32)
    a = np.empty((k // 512, 16))
    for p in range(k // 512):
        a[p, :8] = np.random.permutation(np.resize(levels, 8))
        for g in range(8):
            far = levels[np.abs(levels - a[p, g]) >= 10]
            a[p, g + 8] = far[np.random.randint(len(far))]
    return np.exp2(a.ravel()).repeat(32)


def f64(x):
    return np.asarray(x).astype(np.float64)


def striped8(idx):
    return np.asarray(idx).reshape(8, -1, 16).transpose(0, 2, 1).reshape(128, -1).astype(np.uint16)


def unstriped8(offs):
    return offs.reshape(8, 16, -1).transpose(0, 2, 1).reshape(8, -1).astype(np.int64)


def pick8(x, idx, run):
    r = np.arange(len(x))
    return x[r[:, None], idx[r % (8 * run) // run]]


E2M1 = np.array([0.0, 0.5, 1.0, 1.5, 2.0, 3.0, 4.0, 6.0, -0.0, -0.5, -1.0, -1.5, -2.0, -3.0, -4.0, -6.0])


def pack_weight(w, fmt):
    k, n = w.shape
    w = f64(np.asarray(w, np.float32).astype(ml_dtypes.bfloat16)).reshape(k // 32, 32, n)
    amax = np.abs(w).max(1)
    if fmt == "e4m3":
        byte = np.frexp(amax)[1] - 1 + 127 - 7
    else:
        mant, ex = np.frexp(amax / 6.0)
        byte = np.where(mant > 0.5, ex, ex - 1) + 127
    byte = np.clip(np.where(amax > 0, byte, 1), 1, 254)
    scaled = (w * np.exp2(127.0 - byte)[:, None, :]).reshape(k, n).astype(np.float32)
    by_word = np.ascontiguousarray(scaled.reshape(k // 512, 128, 4, n).transpose(0, 1, 3, 2))
    if fmt == "e4m3":
        words = by_word.astype(ml_dtypes.float8_e4m3fn).view(np.uint8)
    else:
        c = by_word.astype(ml_dtypes.float4_e2m1fn).view(np.uint8) & 0xF
        words = (c[..., 0::2] | (c[..., 1::2] << 4)).reshape(k // 512, 128, 2 * n)
    return np.ascontiguousarray(words), np.ascontiguousarray(byte.astype(np.uint8).reshape(k // 512, 16, n))


def unpack_weight(words, scales, fmt):
    g, _, n = scales.shape
    words = np.ascontiguousarray(words).reshape(g, 128, n, -1)
    if fmt == "e4m3":
        vals = words.view(ml_dtypes.float8_e4m3fn).astype(np.float64)
    else:
        nib = np.empty((g, 128, n, 4), np.uint8)
        nib[..., 0::2] = words & 0xF
        nib[..., 1::2] = words >> 4
        vals = E2M1[nib]
    vals = vals * np.repeat(np.exp2(scales.astype(np.float64) - 127.0), 8, axis=1)[..., None]
    return vals.transpose(0, 1, 3, 2).reshape(g * 512, n)


D, V, Q, I = 512, 2048, 128, 512


def setup_inputs():
    n = np.random.standard_normal
    idx = np.stack([np.random.permutation(V)[:I] for _ in range(8)])
    fd = mx_kscale(D)
    vocp = pack_weight(n((D, V)) / fd[:, None], "e2m1")
    return {
        "hid": (n((D, Q)) * 1.0 / np.sqrt(D) * fd[:, None]).astype(np.float32),
        "voc_words": vocp[0],
        "voc_scales": vocp[1],
        "aim": (np.random.uniform(4.0, 5.5, (Q, 1))).astype(np.float32),
        "old": (0.5 * n((Q, V))).astype(np.float32),
        "offs": striped8(idx),
    }


def reference(hid, voc_words, voc_scales, aim, old, offs):
    idx = unstriped8(offs)
    vocu = unpack_weight(voc_words, voc_scales, "e2m1")
    hidq = mxq(f64(hid), 0, "e4m3")
    a = hidq.T @ vocu
    m1 = np.max(a, axis=1, keepdims=True)
    lx = pick8(a, idx, 16) - m1
    px = np.exp(lx)
    zl = np.sum(px, axis=1, keepdims=True)
    et = np.log(zl) - np.sum(px * lx, axis=1, keepdims=True) / zl
    det = (et - f64(aim)) * 2.0
    dzl = det / zl - det * (-1.0) * np.sum(px * lx, axis=1, keepdims=True) / np.square(zl)
    dpx = det * (-1.0) / zl * lx + dzl
    dlx = det * (-1.0) / zl * px + dpx * px
    s1 = np.zeros((Q, V))
    s1[np.arange(Q)[:, None], idx[np.arange(Q) % 128 // 16]] = dlx
    y = s1 * 256.0 + f64(old)
    return y

@@ -1,0 +1,123 @@
+import math
+from contextlib import ExitStack
+
+import concourse.mybir as mybir
+
+D, V, Q, I = 512, 2048, 128, 512
+FLOPS = 2 * D * V * Q
+
+F32 = mybir.dt.float32
+BF16 = mybir.dt.bfloat16
+I32 = mybir.dt.int32
+U32 = mybir.dt.uint32
+U16 = mybir.dt.uint16
+U8 = mybir.dt.uint8
+FP8X4 = mybir.dt.float8_e4m3fn_x4
+FP4X4 = mybir.dt.float4_e2m1fn_x4
+ALU = mybir.AluOpType
+ACT = mybir.ActivationFunctionType
+
+P = 128
+PACK = 4
+BANK = 512
+PIECES = [512, 512, 512, 512]
+STORES = [256] * 8
+
+
+def tile_attend_blistspread_heads_kernel(tc, hid, voc_words, voc_scales, aim, old, offs, out):
+    nc = tc.nc
+    with ExitStack() as ctx:
+        keep = ctx.enter_context(tc.tile_pool(name="keep", bufs=1))
+        psum = ctx.enter_context(tc.psum_pool(name="psum", bufs=1))
+
+        offsets = keep.tile([P, I // 16], U16, name="offsets")
+        plane = keep.tile([P, V], U8, name="plane", align_bytes=64)
+        nc.vector.memset(plane[:].bitcast(I32), 0)
+        spread = keep.tile([P, V], F32, name="spread")
+        nc.vector.memset(spread[:].bitcast(I32), 0)
+
+        hid_raw = keep.tile([P, PACK, Q], F32, name="hid_raw", tag="wide")
+        nc.sync.dma_start(out=hid_raw[:], in_=hid.rearrange("(p t) q -> p t q", t=PACK))
+        for quad in range(4):
+            nc.scalar.dma_start(
+                out=plane[32 * quad : 32 * quad + 4, :].bitcast(I32),
+                in_=voc_scales[0, 4 * quad : 4 * quad + 4, :].bitcast(I32),
+            )
+        halves = []
+        for h in range(2):
+            words = keep.tile([P, V], U8, name=f"words{h}", align_bytes=64)
+            nc.sync.dma_start(out=words[:].bitcast(I32), in_=voc_words[0, :, h * V : (h + 1) * V].bitcast(I32))
+            halves.append(words)
+        nc.sync.dma_start(offsets[:], offs)
+
+        grouped = keep.tile([P, Q, PACK], BF16, name="grouped", tag="narrow", align_bytes=64)
+        nc.vector.tensor_copy(grouped[:], hid_raw[:].rearrange("p t q -> p q t"))
+        codes = keep.tile([P, Q], U32, name="codes", align_bytes=64)
+        hid_plane = keep.tile([P, Q], U8, name="hid_plane", align_bytes=64)
+        nc.vector.quantize_mx(
+            out=codes[:].bitcast(FP8X4), scales=hid_plane[:], in_=grouped[:].rearrange("p q t -> p (q t)")
+        )
+
+        old_sb = keep.tile([P, V], F32, name="old_sb", tag="wide")
+        nc.sync.dma_start(out=old_sb[:], in_=old)
+        aim_sb = keep.tile([P, 1], F32, name="aim_sb", tag="narrow", align_bytes=64)
+        nc.sync.dma_start(out=aim_sb[:], in_=aim)
+
+        scores = keep.tile([P, V], F32, name="scores")
+        tops = keep.tile([P, len(PIECES)], F32, name="tops")
+        v0 = 0
+        for j, width in enumerate(PIECES):
+            bank = psum.tile([P, width], F32, name=f"bank{j}")
+            h, c0 = divmod(v0, V // 2)
+            nc.tensor.matmul_mx(
+                out=bank[:],
+                lhsT=codes[:].bitcast(FP8X4),
+                lhsT_scale=hid_plane[:],
+                rhs=halves[h][:, 2 * c0 : 2 * (c0 + width)].bitcast(FP4X4),
+                rhs_scale=plane[:, v0 : v0 + width],
+                start=True,
+                stop=True,
+            )
+            nc.vector.tensor_scalar(
+                scores[:, v0 : v0 + width], bank[:], 1.0, None, ALU.mult, ALU.max, accum_out=tops[:, j : j + 1]
+            )
+            v0 = v0 + width
+
+        neg_top = keep.tile([P, 1], F32, name="neg_top")
+        nc.vector.tensor_reduce(neg_top[:], tops[:], mybir.AxisListType.X, ALU.max, negate=True)
+        picked = keep.tile([P, I], F32, name="picked")
+        nc.vector.tensor_copy(picked[:], scores[:].indirect(offsets[:]))
+
+        px = keep.tile([P, I], F32, name="px")
+        zl = keep.tile([P, 1], F32, name="zl")
+        nc.scalar.activation(px[:], picked[:], ACT.Exp, bias=neg_top[:], accum_out=zl[:])
+        lx = keep.tile([P, I], F32, name="lx")
+        nc.vector.tensor_scalar(lx[:], picked[:], neg_top[:], None, ALU.add)
+
+        pl = keep.tile([P, I], F32, name="pl")
+        total = keep.tile([P, 1], F32, name="total")
+        nc.vector.scalar_tensor_tensor(pl[:], lx[:], 1.0, px[:], ALU.mult, ALU.mult, accum_out=total[:])
+        rz = keep.tile([P, 1], F32, name="rz")
+        nc.vector.reciprocal(rz[:], zl[:])
+        centred = keep.tile([P, I], F32, name="centred")
+        nc.vector.tensor_scalar(centred[:], lx[:], zl[:], total[:], ALU.mult, ALU.subtract)
+        nc.vector.tensor_tensor(spread[:].indirect(offsets[:]), px[:], centred[:], ALU.mult)
+
+        log_z = keep.tile([P, 1], F32, name="log_z")
+        nc.scalar.activation(log_z[:], zl[:], ACT.Ln)
+        gap = keep.tile([P, 1], F32, name="gap")
+        nc.scalar.activation(gap[:], log_z[:], ACT.Identity, bias=aim_sb[:], scale=-1.0)
+        miss = keep.tile([P, 1], F32, name="miss")
+        nc.scalar.activation(miss[:], total[:], ACT.Identity, bias=gap[:], scale=rz[:])
+        rz2 = keep.tile([P, 1], F32, name="rz2")
+        nc.scalar.activation(rz2[:], rz[:], ACT.Square, scale=math.sqrt(512.0))
+        coef = keep.tile([P, 1], F32, name="coef")
+        nc.scalar.activation(coef[:], miss[:], ACT.Copy, scale=rz2[:])
+
+        v0 = 0
+        for j, width in enumerate(STORES):
+            cols = slice(v0, v0 + width)
+            result = keep.tile([P, width], F32, name=f"result{j}")
+            nc.vector.scalar_tensor_tensor(result[:], spread[:, cols], coef[:], old_sb[:, cols], ALU.mult, ALU.add)
+            nc.sync.dma_start(out=out[:, cols], in_=result[:])
+            v0 = v0 + width

@@ -20,7 +20,7 @@ ACT = mybir.ActivationFunctionType
 P = 128
 PACK = 4
 BANK = 512
-PIECES = [512, 512, 512, 512]
+PIECES = [256, 256, 512, 512, 512]
 STORES = [256] * 8
 
 
@@ -33,8 +33,6 @@ def tile_attend_blistspread_heads_kernel(tc, hid, voc_words, voc_scales, aim, ol
         offsets = keep.tile([P, I // 16], U16, name="offsets")
         plane = keep.tile([P, V], U8, name="plane", align_bytes=64)
         nc.vector.memset(plane[:].bitcast(I32), 0)
-        spread = keep.tile([P, V], F32, name="spread")
-        nc.vector.memset(spread[:].bitcast(I32), 0)
 
         hid_raw = keep.tile([P, PACK, Q], F32, name="hid_raw", tag="wide")
         nc.sync.dma_start(out=hid_raw[:], in_=hid.rearrange("(p t) q -> p t q", t=PACK))
@@ -51,8 +49,11 @@ def tile_attend_blistspread_heads_kernel(tc, hid, voc_words, voc_scales, aim, ol
         nc.sync.dma_start(offsets[:], offs)
 
         grouped = keep.tile([P, Q, PACK], BF16, name="grouped", tag="narrow", align_bytes=64)
-        nc.vector.tensor_copy(grouped[:], hid_raw[:].rearrange("p t q -> p q t"))
-        codes = keep.tile([P, Q], U32, name="codes", align_bytes=64)
+        nc.vector.tensor_copy(
+            grouped[:].rearrange("p (c i) t -> p c t i", i=4),
+            hid_raw[:].rearrange("p t (c i) -> p c t i", i=4),
+        )
+        codes = keep.tile([P, Q], U32, name="codes", tag="late", align_bytes=64)
         hid_plane = keep.tile([P, Q], U8, name="hid_plane", align_bytes=64)
         nc.vector.quantize_mx(
             out=codes[:].bitcast(FP8X4), scales=hid_plane[:], in_=grouped[:].rearrange("p q t -> p (q t)")
@@ -60,8 +61,8 @@ def tile_attend_blistspread_heads_kernel(tc, hid, voc_words, voc_scales, aim, ol
 
         old_sb = keep.tile([P, V], F32, name="old_sb", tag="wide")
         nc.sync.dma_start(out=old_sb[:], in_=old)
-        aim_sb = keep.tile([P, 1], F32, name="aim_sb", tag="narrow", align_bytes=64)
-        nc.sync.dma_start(out=aim_sb[:], in_=aim)
+        spread = keep.tile([P, V], F32, name="spread", tag="narrow", align_bytes=64)
+        nc.gpsimd.memset(spread[:], 0.0)
 
         scores = keep.tile([P, V], F32, name="scores")
         tops = keep.tile([P, len(PIECES)], F32, name="tops")
@@ -83,6 +84,8 @@ def tile_attend_blistspread_heads_kernel(tc, hid, voc_words, voc_scales, aim, ol
             )
             v0 = v0 + width
 
+        aim_sb = keep.tile([P, 1], F32, name="aim_sb", tag="late", align_bytes=64)
+        nc.sync.dma_start(out=aim_sb[:], in_=aim)
         neg_top = keep.tile([P, 1], F32, name="neg_top")
         nc.vector.tensor_reduce(neg_top[:], tops[:], mybir.AxisListType.X, ALU.max, negate=True)
         picked = keep.tile([P, I], F32, name="picked")

@@ -21,6 +21,7 @@ P = 128
 PACK = 4
 BANK = 512
 PIECES = [256, 256, 512, 512, 512]
+SPLIT = 80
 STORES = [256] * 8
 
 
@@ -32,12 +33,14 @@ def tile_attend_blistspread_heads_kernel(tc, hid, voc_words, voc_scales, aim, ol
 
         offsets = keep.tile([P, I // 16], U16, name="offsets")
         plane = keep.tile([P, V], U8, name="plane", align_bytes=64)
-        nc.vector.memset(plane[:].bitcast(I32), 0)
+        nc.vector.memset(plane[:, : V // 2].bitcast(I32), 0)
+        nc.gpsimd.memset(plane[:, V // 2 :].bitcast(I32), 0)
 
         hid_raw = keep.tile([P, PACK, Q], F32, name="hid_raw", tag="wide")
         nc.sync.dma_start(out=hid_raw[:], in_=hid.rearrange("(p t) q -> p t q", t=PACK))
+        nc.sync.dma_start(offsets[:], offs)
         for quad in range(4):
-            nc.scalar.dma_start(
+            nc.sync.dma_start(
                 out=plane[32 * quad : 32 * quad + 4, :].bitcast(I32),
                 in_=voc_scales[0, 4 * quad : 4 * quad + 4, :].bitcast(I32),
             )
@@ -46,12 +49,15 @@ def tile_attend_blistspread_heads_kernel(tc, hid, voc_words, voc_scales, aim, ol
             words = keep.tile([P, V], U8, name=f"words{h}", align_bytes=64)
             nc.sync.dma_start(out=words[:].bitcast(I32), in_=voc_words[0, :, h * V : (h + 1) * V].bitcast(I32))
             halves.append(words)
-        nc.sync.dma_start(offsets[:], offs)
 
         grouped = keep.tile([P, Q, PACK], BF16, name="grouped", tag="narrow", align_bytes=64)
         nc.vector.tensor_copy(
-            grouped[:].rearrange("p (c i) t -> p c t i", i=4),
-            hid_raw[:].rearrange("p t (c i) -> p c t i", i=4),
+            grouped[:, :SPLIT, :].rearrange("p (c i) t -> p c t i", i=4),
+            hid_raw[:, :, :SPLIT].rearrange("p t (c i) -> p c t i", i=4),
+        )
+        nc.scalar.copy(
+            grouped[:, SPLIT:, :].rearrange("p (c i) t -> p c t i", i=4),
+            hid_raw[:, :, SPLIT:].rearrange("p t (c i) -> p c t i", i=4),
         )
         codes = keep.tile([P, Q], U32, name="codes", tag="late", align_bytes=64)
         hid_plane = keep.tile([P, Q], U8, name="hid_plane", align_bytes=64)

@@ -22,7 +22,8 @@ PACK = 4
 BANK = 512
 PIECES = [256, 256, 512, 512, 512]
 SPLIT = 80
-STORES = [256] * 8
+LOADS = [512, 512, 1024]
+STORES = [128] + [256] * 7 + [128]
 
 
 def tile_attend_blistspread_heads_kernel(tc, hid, voc_words, voc_scales, aim, old, offs, out):
@@ -38,18 +39,20 @@ def tile_attend_blistspread_heads_kernel(tc, hid, voc_words, voc_scales, aim, ol
 
         hid_raw = keep.tile([P, PACK, Q], F32, name="hid_raw", tag="wide")
         nc.sync.dma_start(out=hid_raw[:], in_=hid.rearrange("(p t) q -> p t q", t=PACK))
-        nc.sync.dma_start(offsets[:], offs)
         for quad in range(4):
             nc.sync.dma_start(
                 out=plane[32 * quad : 32 * quad + 4, :].bitcast(I32),
                 in_=voc_scales[0, 4 * quad : 4 * quad + 4, :].bitcast(I32),
             )
-        halves = []
-        for h in range(2):
-            words = keep.tile([P, V], U8, name=f"words{h}", align_bytes=64)
-            nc.sync.dma_start(out=words[:].bitcast(I32), in_=voc_words[0, :, h * V : (h + 1) * V].bitcast(I32))
-            halves.append(words)
+        loads = []
+        v0 = 0
+        for h, width in enumerate(LOADS):
+            words = keep.tile([P, 2 * width], U8, name=f"words{h}", align_bytes=64)
+            nc.sync.dma_start(out=words[:].bitcast(I32), in_=voc_words[0, :, 2 * v0 : 2 * (v0 + width)].bitcast(I32))
+            loads.append((v0, words))
+            v0 = v0 + width
 
+        nc.sync.dma_start(offsets[:], offs)
         grouped = keep.tile([P, Q, PACK], BF16, name="grouped", tag="narrow", align_bytes=64)
         nc.vector.tensor_copy(
             grouped[:, :SPLIT, :].rearrange("p (c i) t -> p c t i", i=4),
@@ -75,12 +78,13 @@ def tile_attend_blistspread_heads_kernel(tc, hid, voc_words, voc_scales, aim, ol
         v0 = 0
         for j, width in enumerate(PIECES):
             bank = psum.tile([P, width], F32, name=f"bank{j}")
-            h, c0 = divmod(v0, V // 2)
+            first, words = [load for load in loads if load[0] <= v0][-1]
+            c0 = v0 - first
             nc.tensor.matmul_mx(
                 out=bank[:],
                 lhsT=codes[:].bitcast(FP8X4),
                 lhsT_scale=hid_plane[:],
-                rhs=halves[h][:, 2 * c0 : 2 * (c0 + width)].bitcast(FP4X4),
+                rhs=words[:, 2 * c0 : 2 * (c0 + width)].bitcast(FP4X4),
                 rhs_scale=plane[:, v0 : v0 + width],
                 start=True,
                 stop=True,

import math
from contextlib import ExitStack

import concourse.mybir as mybir

D, V, Q, I = 512, 2048, 128, 512
FLOPS = 2 * D * V * Q

F32 = mybir.dt.float32
BF16 = mybir.dt.bfloat16
I32 = mybir.dt.int32
U32 = mybir.dt.uint32
U16 = mybir.dt.uint16
U8 = mybir.dt.uint8
FP8X4 = mybir.dt.float8_e4m3fn_x4
FP4X4 = mybir.dt.float4_e2m1fn_x4
ALU = mybir.AluOpType
ACT = mybir.ActivationFunctionType

P = 128
PACK = 4
BANK = 512
PIECES = [256, 256, 512, 512, 512]
SPLIT = 80
LOADS = [512, 512, 1024]
STORES = [128] + [256] * 7 + [128]


def tile_attend_blistspread_heads_kernel(tc, hid, voc_words, voc_scales, aim, old, offs, out):
    nc = tc.nc
    with ExitStack() as ctx:
        keep = ctx.enter_context(tc.tile_pool(name="keep", bufs=1))
        psum = ctx.enter_context(tc.psum_pool(name="psum", bufs=1))

        offsets = keep.tile([P, I // 16], U16, name="offsets")
        plane = keep.tile([P, V], U8, name="plane", align_bytes=64)
        nc.vector.memset(plane[:, : V // 2].bitcast(I32), 0)
        nc.gpsimd.memset(plane[:, V // 2 :].bitcast(I32), 0)

        hid_raw = keep.tile([P, PACK, Q], F32, name="hid_raw", tag="wide")
        nc.sync.dma_start(out=hid_raw[:], in_=hid.rearrange("(p t) q -> p t q", t=PACK))
        for quad in range(4):
            nc.sync.dma_start(
                out=plane[32 * quad : 32 * quad + 4, :].bitcast(I32),
                in_=voc_scales[0, 4 * quad : 4 * quad + 4, :].bitcast(I32),
            )
        loads = []
        v0 = 0
        for h, width in enumerate(LOADS):
            words = keep.tile([P, 2 * width], U8, name=f"words{h}", align_bytes=64)
            nc.sync.dma_start(out=words[:].bitcast(I32), in_=voc_words[0, :, 2 * v0 : 2 * (v0 + width)].bitcast(I32))
            loads.append((v0, words))
            v0 = v0 + width

        nc.sync.dma_start(offsets[:], offs)
        grouped = keep.tile([P, Q, PACK], BF16, name="grouped", tag="narrow", align_bytes=64)
        nc.vector.tensor_copy(
            grouped[:, :SPLIT, :].rearrange("p (c i) t -> p c t i", i=4),
            hid_raw[:, :, :SPLIT].rearrange("p t (c i) -> p c t i", i=4),
        )
        nc.scalar.copy(
            grouped[:, SPLIT:, :].rearrange("p (c i) t -> p c t i", i=4),
            hid_raw[:, :, SPLIT:].rearrange("p t (c i) -> p c t i", i=4),
        )
        codes = keep.tile([P, Q], U32, name="codes", tag="late", align_bytes=64)
        hid_plane = keep.tile([P, Q], U8, name="hid_plane", align_bytes=64)
        nc.vector.quantize_mx(
            out=codes[:].bitcast(FP8X4), scales=hid_plane[:], in_=grouped[:].rearrange("p q t -> p (q t)")
        )

        old_sb = keep.tile([P, V], F32, name="old_sb", tag="wide")
        nc.sync.dma_start(out=old_sb[:], in_=old)
        spread = keep.tile([P, V], F32, name="spread", tag="narrow", align_bytes=64)
        nc.gpsimd.memset(spread[:], 0.0)

        scores = keep.tile([P, V], F32, name="scores")
        tops = keep.tile([P, len(PIECES)], F32, name="tops")
        v0 = 0
        for j, width in enumerate(PIECES):
            bank = psum.tile([P, width], F32, name=f"bank{j}")
            first, words = [load for load in loads if load[0] <= v0][-1]
            c0 = v0 - first
            nc.tensor.matmul_mx(
                out=bank[:],
                lhsT=codes[:].bitcast(FP8X4),
                lhsT_scale=hid_plane[:],
                rhs=words[:, 2 * c0 : 2 * (c0 + width)].bitcast(FP4X4),
                rhs_scale=plane[:, v0 : v0 + width],
                start=True,
                stop=True,
            )
            nc.vector.tensor_scalar(
                scores[:, v0 : v0 + width], bank[:], 1.0, None, ALU.mult, ALU.max, accum_out=tops[:, j : j + 1]
            )
            v0 = v0 + width

        aim_sb = keep.tile([P, 1], F32, name="aim_sb", tag="late", align_bytes=64)
        nc.sync.dma_start(out=aim_sb[:], in_=aim)
        neg_top = keep.tile([P, 1], F32, name="neg_top")
        nc.vector.tensor_reduce(neg_top[:], tops[:], mybir.AxisListType.X, ALU.max, negate=True)
        picked = keep.tile([P, I], F32, name="picked")
        nc.vector.tensor_copy(picked[:], scores[:].indirect(offsets[:]))

        px = keep.tile([P, I], F32, name="px")
        zl = keep.tile([P, 1], F32, name="zl")
        nc.scalar.activation(px[:], picked[:], ACT.Exp, bias=neg_top[:], accum_out=zl[:])
        lx = keep.tile([P, I], F32, name="lx")
        nc.vector.tensor_scalar(lx[:], picked[:], neg_top[:], None, ALU.add)

        pl = keep.tile([P, I], F32, name="pl")
        total = keep.tile([P, 1], F32, name="total")
        nc.vector.scalar_tensor_tensor(pl[:], lx[:], 1.0, px[:], ALU.mult, ALU.mult, accum_out=total[:])
        rz = keep.tile([P, 1], F32, name="rz")
        nc.vector.reciprocal(rz[:], zl[:])
        centred = keep.tile([P, I], F32, name="centred")
        nc.vector.tensor_scalar(centred[:], lx[:], zl[:], total[:], ALU.mult, ALU.subtract)
        nc.vector.tensor_tensor(spread[:].indirect(offsets[:]), px[:], centred[:], ALU.mult)

        log_z = keep.tile([P, 1], F32, name="log_z")
        nc.scalar.activation(log_z[:], zl[:], ACT.Ln)
        gap = keep.tile([P, 1], F32, name="gap")
        nc.scalar.activation(gap[:], log_z[:], ACT.Identity, bias=aim_sb[:], scale=-1.0)
        miss = keep.tile([P, 1], F32, name="miss")
        nc.scalar.activation(miss[:], total[:], ACT.Identity, bias=gap[:], scale=rz[:])
        rz2 = keep.tile([P, 1], F32, name="rz2")
        nc.scalar.activation(rz2[:], rz[:], ACT.Square, scale=math.sqrt(512.0))
        coef = keep.tile([P, 1], F32, name="coef")
        nc.scalar.activation(coef[:], miss[:], ACT.Copy, scale=rz2[:])

        v0 = 0
        for j, width in enumerate(STORES):
            cols = slice(v0, v0 + width)
            result = keep.tile([P, width], F32, name=f"result{j}")
            nc.vector.scalar_tensor_tensor(result[:], spread[:, cols], coef[:], old_sb[:, cols], ALU.mult, ALU.add)
            nc.sync.dma_start(out=out[:, cols], in_=result[:])
            v0 = v0 + width
